import numpy as np
import ml_dtypes


def mxq(x, axis, fmt="e4m3"):
    dtype, down = {"e4m3": (ml_dtypes.float8_e4m3fn, 7), "e5m2": (ml_dtypes.float8_e5m2, 14)}[fmt]
    v = np.moveaxis(np.asarray(x, np.float32).astype(ml_dtypes.bfloat16).astype(np.float64), axis, -1)
    blocks = v.reshape(v.shape[:-1] + (-1, 32))
    amax = np.abs(blocks).max(-1, keepdims=True)
    byte = np.maximum(np.where(amax > 0, np.frexp(amax)[1] - 1 + 127, 0) - down, 1)
    scale = np.exp2(byte - 127.0)
    codes = (blocks / scale).astype(np.float32).astype(dtype).astype(np.float64)
    return np.moveaxis((codes * scale).reshape(v.shape), -1, axis)


WIDE = False


def mx_kscale(k):
    if not WIDE:
        return np.ones(k)
    levels = np.array([10, -10, 5, -5, 0])
    if k % 512:
        return np.exp2(np.random.permutation(np.resize(levels, k // 32))).repeat(32)
    a = np.empty((k // 512, 16))
    for p in range(k // 512):
        a[p, :8] = np.random.permutation(np.resize(levels, 8))
        for g in range(8):
            far = levels[np.abs(levels - a[p, g]) >= 10]
            a[p, g + 8] = far[np.random.randint(len(far))]
    return np.exp2(a.ravel()).repeat(32)


def f64(x):
    return np.asarray(x).astype(np.float64)


def striped(idx):
    return np.tile(idx.reshape(-1, 16).T, (8, 1)).astype(np.uint16)


def unstriped(offs):
    return offs[:16].T.reshape(-1).astype(np.int64)


def striped8(idx):
    return np.concatenate([x.reshape(-1, 16).T for x in idx]).astype(np.uint16)


def runs(offs, k):
    lists = np.stack([offs[16 * r : 16 * r + 16].T.reshape(-1) for r in range(8)]).astype(np.int64)
    return lists[np.arange(k) % 512 // 64]


def pack_weight(w):
    k, n = w.shape
    w = f64(np.asarray(w, np.float32).astype(ml_dtypes.bfloat16)).reshape(k // 32, 32, n)
    amax = np.abs(w).max(1)
    byte = np.clip(np.where(amax > 0, np.frexp(amax)[1] - 1 + 127 - 7, 1), 1, 254)
    scaled = (w * np.exp2(127.0 - byte)[:, None, :]).reshape(k, n).astype(np.float32)
    words = np.ascontiguousarray(scaled.reshape(k // 512, 128, 4, n).transpose(0, 1, 3, 2)).astype(ml_dtypes.float8_e4m3fn).view(np.uint8)
    return words, np.ascontiguousarray(byte.astype(np.uint8).reshape(k // 512, 16, n))


def unpack_weight(words, scales):
    g, p, n, _ = words.shape
    vals = np.ascontiguousarray(words).view(ml_dtypes.float8_e4m3fn).astype(np.float64) * np.repeat(np.exp2(scales.astype(np.float64) - 127.0), 8, axis=1)[..., None]
    return vals.transpose(0, 1, 3, 2).reshape(g * 512, n)


def relu(v):
    return np.maximum(v, 0.0)

def planes(y):
    n, m = y.shape
    v = y.astype(np.float32).astype(ml_dtypes.bfloat16).astype(np.float64).reshape(n // 32, 32, m)
    top = np.abs(v).max(1)
    byte = np.clip(np.where(top > 0, np.frexp(top)[1] - 1 + 127 - 7, 1), 1, 254)
    codes = (v * np.exp2(127.0 - byte)[:, None, :]).reshape(n, m).astype(np.float32).astype(ml_dtypes.float8_e4m3fn).view(np.uint8)
    words = codes.reshape(n // 512, 128, 4, m).transpose(0, 1, 3, 2)
    return np.ascontiguousarray(words), np.ascontiguousarray(byte.astype(np.uint8).reshape(n // 512, 16, m))


K, T, S, V, H = 512, 2048, 512, 512, 512


def setup_inputs():
    n = np.random.standard_normal
    s = mx_kscale(K)[:, None]
    packed_xT = pack_weight(n((K, T)) * s)
    packed_w1 = pack_weight(n((K, H)) / np.sqrt(K) / s)
    return {
        "x_words": packed_xT[0],
        "x_scales": packed_xT[1],
        "w1_words": packed_w1[0],
        "w1_scales": packed_w1[1],
        "gs": (np.random.uniform(0.5, 1.5, (K, 1)) / s).astype(np.float32),
        "offs": striped(np.random.permutation(T)[:S]),
        "cand": striped(np.random.permutation(T)[:V]),
        "neg": striped8(np.stack([np.random.permutation(S) for _ in range(8)])),
    }


def reference(x_words, x_scales, w1_words, w1_scales, gs, offs, cand, neg):
    x_cand = unpack_weight(x_words, x_scales)[:, unstriped(cand)]
    xq = unpack_weight(x_words, x_scales)[:, unstriped(offs)]
    h = relu(unpack_weight(w1_words, w1_scales).T @ xq)
    z = f64(gs) * h
    s = 0.0625 * ((x_cand.T @ mxq(z, 0, "e4m3")))
    out_0 = relu(s[np.arange(V)[:, None], runs(neg, V)] - s + 1)
    return (out_0,) + planes(out_0)

@@ -1,0 +1,179 @@
+from contextlib import ExitStack
+
+import concourse.mybir as mybir
+
+K, T, S, V, H = 512, 2048, 512, 512, 512
+FLOPS = 2 * K * H * S + 2 * H * V * S
+
+F32 = mybir.dt.float32
+BF16 = mybir.dt.bfloat16
+I32 = mybir.dt.int32
+U32 = mybir.dt.uint32
+U16 = mybir.dt.uint16
+U8 = mybir.dt.uint8
+FP8X4 = mybir.dt.float8_e4m3fn_x4
+ALU = mybir.AluOpType
+ACT = mybir.ActivationFunctionType
+
+P = 128
+PACK = 4
+CH = 128
+NCH = S // CH
+PIECES = ((0, 256), (256, 128), (384, 128))
+
+
+def tile_picked_candhinge_none_po_kernel(
+    tc, x_words, x_scales, w1_words, w1_scales, gs, offs, cand, neg, out_0, out_1, out_2
+):
+    nc = tc.nc
+    with ExitStack() as ctx:
+        lists = ctx.enter_context(tc.tile_pool(name="lists", bufs=1))
+        sb = ctx.enter_context(tc.tile_pool(name="sb", bufs=1))
+        psum = ctx.enter_context(tc.psum_pool(name="psum", bufs=1))
+
+        offs_sb = lists.tile([P, S // 16], U16, name="offs_sb")
+        cand_sb = lists.tile([P, V // 16], U16, name="cand_sb")
+        neg_sb = lists.tile([P, S // 16], U16, name="neg_sb")
+
+        xw = sb.tile([P, T], I32, name="xw", align_bytes=64)
+        xs = sb.tile([P, T], U8, name="xs", align_bytes=64)
+        ww_raw = sb.tile([P, H], I32, name="ww_raw", align_bytes=64)
+        ws_raw = sb.tile([P, H], U8, name="ws_raw", tag="late", align_bytes=64)
+        gs_sb = sb.tile([P, 1, PACK], F32, name="gs_sb")
+
+        nc.vector.memset(xs[:].bitcast(I32), 0)
+        nc.vector.memset(ws_raw[:].bitcast(I32), 0)
+
+        nc.sync.dma_start(cand_sb[:], cand)
+        nc.sync.dma_start(offs_sb[:], offs)
+        nc.sync.dma_start(neg_sb[:], neg)
+        for q in range(4):
+            eng = nc.sync if q < 2 else nc.scalar
+            eng.dma_start(xs[32 * q : 32 * q + 4, :].bitcast(I32), x_scales[0, 4 * q : 4 * q + 4, :].bitcast(I32))
+        nc.sync.dma_start(xw[:], x_words[0].rearrange("p n t -> p (n t)").bitcast(I32))
+        nc.sync.dma_start(ww_raw[:], w1_words[0].rearrange("p n t -> p (n t)").bitcast(I32))
+        for q in range(4):
+            nc.sync.dma_start(ws_raw[32 * q : 32 * q + 4, :].bitcast(I32), w1_scales[0, 4 * q : 4 * q + 4, :].bitcast(I32))
+        nc.sync.dma_start(gs_sb[:, 0, :], gs.rearrange("(p t) o -> p (t o)", t=PACK))
+
+        def deal_words(dst, src):
+            nc.vector.tensor_copy(
+                dst.rearrange("p (t a i) -> p a t i", t=PACK, i=4), src.rearrange("p (a i t) -> p a t i", t=PACK, i=4)
+            )
+
+        def deal_bytes(dst, src):
+            nc.vector.tensor_copy(
+                dst.rearrange("p (t a i) -> p a t i", t=PACK, i=16), src.rearrange("p (a i t) -> p a t i", t=PACK, i=16)
+            )
+
+        qs = sb.tile([P, S], U8, name="qs", align_bytes=64)
+        cs_raw = sb.tile([P, V], U8, name="cs_raw", align_bytes=64)
+        cs = sb.tile([P, V], U8, name="cs", align_bytes=64)
+        ww = sb.tile([P, H], I32, name="ww", align_bytes=64)
+        ws = sb.tile([P, H], U8, name="ws", align_bytes=64)
+        qw = sb.tile([P, S], U32, name="qw", align_bytes=64)
+
+        nc.vector.tensor_copy(cs_raw[:], xs[:].indirect(cand_sb[:]))
+        nc.vector.tensor_copy(qs[:], xs[:].indirect(offs_sb[:]))
+        deal_bytes(cs[:], cs_raw[:])
+        nc.vector.tensor_copy(qw[:], xw[:].bitcast(U32).indirect(offs_sb[:]))
+        deal_words(ww[:], ww_raw[:])
+        deal_bytes(ws[:], ws_raw[:])
+        cw = sb.tile([P, V], U32, name="cw", tag="late", align_bytes=64)
+        nc.vector.tensor_copy(cw[:].rearrange("p (t m) -> p m t", t=PACK), xw[:].bitcast(U32).indirect(cand_sb[:]))
+
+        hb = [psum.tile([P, PACK, CH], F32, name=f"hb{c}") for c in range(NCH)]
+        sbk = [psum.tile([P, PACK, CH], F32, name=f"sbk{c}") for c in range(NCH)]
+        for c in range(NCH):
+            cols = slice(c * CH, (c + 1) * CH)
+            for t in range(PACK):
+                m = slice(t * P, (t + 1) * P)
+                nc.tensor.matmul_mx(
+                    out=hb[c][:, t, :], lhsT=ww[:, m].bitcast(FP8X4), lhsT_scale=ws[:, m],
+                    rhs=qw[:, cols].bitcast(FP8X4), rhs_scale=qs[:, cols], start=True, stop=True,
+                )
+
+        zb = [sb.tile([P, CH, PACK], BF16, name=f"zb{c}", align_bytes=64) for c in range(NCH)]
+        zw = [sb.tile([P, CH], U32, name=f"zw{c}", align_bytes=64) for c in range(NCH)]
+        zs = [sb.tile([P, CH], U8, name=f"zs{c}", align_bytes=64) for c in range(NCH)]
+        win = [sb.tile([P, S], F32, name=f"win{t}", align_bytes=64) for t in range(PACK)]
+        own = [sb.tile([P, PACK, n], F32, name=f"own{i}", align_bytes=64) for i, (j0, n) in enumerate(PIECES)]
+
+        def make_z(c):
+            nc.vector.scalar_tensor_tensor(
+                zb[c][:], hb[c][:].rearrange("p t n -> p n t"), 0.0, gs_sb[:].to_broadcast([P, CH, PACK]), ALU.max, ALU.mult
+            )
+
+        def score(c):
+            nc.vector.quantize_mx(zw[c][:].bitcast(FP8X4), zs[c][:], zb[c][:].rearrange("p n t -> p (n t)"))
+            for t in range(PACK):
+                m = slice(t * P, (t + 1) * P)
+                nc.tensor.matmul_mx(
+                    out=sbk[c][:, t, :], lhsT=cw[:, m].bitcast(FP8X4), lhsT_scale=cs[:, m],
+                    rhs=zw[c][:].bitcast(FP8X4), rhs_scale=zs[c][:], start=True, stop=True,
+                )
+            for t in range(PACK):
+                nc.scalar.activation(win[t][:, c * CH : (c + 1) * CH], sbk[c][:, t, :], ACT.Copy, scale=0.0625)
+
+        make_z(0)
+        for c in range(NCH):
+            if c + 1 < NCH:
+                make_z(c + 1)
+            score(c)
+
+        nc.vector.tensor_scalar(own[0][:, :, 0:CH], sbk[0][:], 0.0625, None, ALU.mult)
+        nc.vector.tensor_scalar(own[0][:, :, CH : 2 * CH], sbk[1][:], 0.0625, None, ALU.mult)
+        nc.scalar.activation(own[1][:], sbk[2][:], ACT.Copy, scale=0.0625)
+        nc.scalar.activation(own[2][:], sbk[3][:], ACT.Copy, scale=0.0625)
+
+        ys = sb.tile([P, S], U8, name="ys", align_bytes=64)
+        out_rows = out_0.rearrange("(p t) j -> p t j", t=PACK)
+        out_words = out_1[0].rearrange("p n t -> p (n t)").bitcast(I32)
+        d, y, yb, yw = [], [], [], []
+        for i, (j0, n) in enumerate(PIECES):
+            d.append(sb.tile([P, PACK, n], F32, name=f"d{i}", align_bytes=64))
+            y.append(sb.tile([P, PACK, n], F32, name=f"y{i}", align_bytes=64))
+            yb.append(sb.tile([P, n, PACK], BF16, name=f"yb{i}", align_bytes=64))
+            yw.append(sb.tile([P, n], I32, name=f"yw{i}", align_bytes=64))
+
+        def fetch(i):
+            j0, n = PIECES[i]
+            for t in range(PACK):
+                nc.vector.tensor_tensor(
+                    d[i][:, t, :], win[t][:].indirect(neg_sb[:, j0 // 16 : (j0 + n) // 16]), own[i][:, t, :], ALU.subtract
+                )
+
+        def hinge(i, t0=0, t1=PACK):
+            j0, n = PIECES[i]
+            nc.scalar.activation(y[i][:, t0:t1, :], d[i][:, t0:t1, :], ACT.Relu, bias=1.0)
+            nc.sync.dma_start(out_rows[:, t0:t1, j0 : j0 + n], y[i][:, t0:t1, :])
+
+        def weave(i, on_vector):
+            dst = yb[i][:].rearrange("p (a i) t -> p a t i", i=4)
+            src = d[i][:].rearrange("p t (a i) -> p a t i", i=4)
+            if on_vector:
+                nc.vector.tensor_scalar(dst, src, 1.0, 0.0, ALU.add, ALU.max)
+            else:
+                nc.scalar.activation(dst, src, ACT.Relu, bias=1.0)
+
+        def pack(i):
+            j0, n = PIECES[i]
+            nc.vector.quantize_mx(yw[i][:].bitcast(FP8X4), ys[:, j0 : j0 + n], yb[i][:].rearrange("p n t -> p (n t)"))
+            nc.sync.dma_start(out_words[:, j0 : j0 + n], yw[i][:])
+
+        fetch(0)
+        hinge(0, 0, 2)
+        hinge(0, 2, 4)
+        weave(0, False)
+        fetch(1)
+        hinge(1)
+        fetch(2)
+        hinge(2)
+        weave(1, True)
+        pack(0)
+        weave(2, True)
+        pack(1)
+        pack(2)
+        for q in range(4):
+            eng = nc.scalar if q % 2 else nc.sync
+            eng.dma_start(out_2[0, 4 * q : 4 * q + 4, :].bitcast(I32), ys[32 * q : 32 * q + 4, :].bitcast(I32))

@@ -19,7 +19,7 @@ P = 128
 PACK = 4
 CH = 128
 NCH = S // CH
-PIECES = ((0, 256), (256, 128), (384, 128))
+HALF = S // 2
 
 
 def tile_picked_candhinge_none_po_kernel(
@@ -82,8 +82,7 @@ def tile_picked_candhinge_none_po_kernel(
         cw = sb.tile([P, V], U32, name="cw", tag="late", align_bytes=64)
         nc.vector.tensor_copy(cw[:].rearrange("p (t m) -> p m t", t=PACK), xw[:].bitcast(U32).indirect(cand_sb[:]))
 
-        hb = [psum.tile([P, PACK, CH], F32, name=f"hb{c}") for c in range(NCH)]
-        sbk = [psum.tile([P, PACK, CH], F32, name=f"sbk{c}") for c in range(NCH)]
+        hb = [psum.tile([P, PACK, CH], F32, name=f"hb{c}", tag=f"hb{c}") for c in range(NCH)]
         for c in range(NCH):
             cols = slice(c * CH, (c + 1) * CH)
             for t in range(PACK):
@@ -97,7 +96,8 @@ def tile_picked_candhinge_none_po_kernel(
         zw = [sb.tile([P, CH], U32, name=f"zw{c}", align_bytes=64) for c in range(NCH)]
         zs = [sb.tile([P, CH], U8, name=f"zs{c}", align_bytes=64) for c in range(NCH)]
         win = [sb.tile([P, S], F32, name=f"win{t}", align_bytes=64) for t in range(PACK)]
-        own = [sb.tile([P, PACK, n], F32, name=f"own{i}", align_bytes=64) for i, (j0, n) in enumerate(PIECES)]
+        own = [[sb.tile([P, HALF], F32, name=f"own{h}_{t}", tag=f"own{h}_{t}", align_bytes=64) for t in range(PACK)] for h in range(2)]
+        acc = {}
 
         def make_z(c):
             nc.vector.scalar_tensor_tensor(
@@ -106,74 +106,81 @@ def tile_picked_candhinge_none_po_kernel(
 
         def score(c):
             nc.vector.quantize_mx(zw[c][:].bitcast(FP8X4), zs[c][:], zb[c][:].rearrange("p n t -> p (n t)"))
+            if c + 1 < NCH:
+                bank = psum.tile([P, PACK, CH], F32, name=f"sbk{c}")
             for t in range(PACK):
+                if c + 1 < NCH:
+                    acc[c, t] = bank[:, t, :]
+                else:
+                    last = psum.tile([P, CH], F32, name=f"last{t}", tag=f"hb{t}")
+                    acc[c, t] = last[:]
                 m = slice(t * P, (t + 1) * P)
                 nc.tensor.matmul_mx(
-                    out=sbk[c][:, t, :], lhsT=cw[:, m].bitcast(FP8X4), lhsT_scale=cs[:, m],
+                    out=acc[c, t], lhsT=cw[:, m].bitcast(FP8X4), lhsT_scale=cs[:, m],
                     rhs=zw[c][:].bitcast(FP8X4), rhs_scale=zs[c][:], start=True, stop=True,
                 )
-            for t in range(PACK):
-                nc.scalar.activation(win[t][:, c * CH : (c + 1) * CH], sbk[c][:, t, :], ACT.Copy, scale=0.0625)
+
+        def drain(c, t):
+            nc.scalar.activation(win[t][:, c * CH : (c + 1) * CH], acc[c, t], ACT.Copy, scale=0.0625)
 
         make_z(0)
         for c in range(NCH):
             if c + 1 < NCH:
                 make_z(c + 1)
             score(c)
-
-        nc.vector.tensor_scalar(own[0][:, :, 0:CH], sbk[0][:], 0.0625, None, ALU.mult)
-        nc.vector.tensor_scalar(own[0][:, :, CH : 2 * CH], sbk[1][:], 0.0625, None, ALU.mult)
-        nc.scalar.activation(own[1][:], sbk[2][:], ACT.Copy, scale=0.0625)
-        nc.scalar.activation(own[2][:], sbk[3][:], ACT.Copy, scale=0.0625)
+        for c in range(2):
+            for t in range(PACK):
+                drain(c, t)
+        for t in range(PACK):
+            nc.vector.tensor_copy(own[0][t][:], win[t][:, 0:HALF])
+        for t in range(PACK):
+            drain(2, t)
+            drain(3, t)
+            nc.sync.dma_start(own[1][t][:], win[t][:, HALF:S])
 
         ys = sb.tile([P, S], U8, name="ys", align_bytes=64)
         out_rows = out_0.rearrange("(p t) j -> p t j", t=PACK)
         out_words = out_1[0].rearrange("p n t -> p (n t)").bitcast(I32)
-        d, y, yb, yw = [], [], [], []
-        for i, (j0, n) in enumerate(PIECES):
-            d.append(sb.tile([P, PACK, n], F32, name=f"d{i}", align_bytes=64))
-            y.append(sb.tile([P, PACK, n], F32, name=f"y{i}", align_bytes=64))
-            yb.append(sb.tile([P, n, PACK], BF16, name=f"yb{i}", align_bytes=64))
-            yw.append(sb.tile([P, n], I32, name=f"yw{i}", align_bytes=64))
+        d = [sb.tile([P, PACK, HALF], F32, name=f"d{h}", align_bytes=64) for h in range(2)]
+        y = [sb.tile([P, PACK, HALF], F32, name=f"y{h}", align_bytes=64) for h in range(2)]
 
-        def fetch(i):
-            j0, n = PIECES[i]
+        def fetch(h):
             for t in range(PACK):
                 nc.vector.tensor_tensor(
-                    d[i][:, t, :], win[t][:].indirect(neg_sb[:, j0 // 16 : (j0 + n) // 16]), own[i][:, t, :], ALU.subtract
+                    d[h][:, t, :], win[t][:].indirect(neg_sb[:, h * HALF // 16 : (h + 1) * HALF // 16]), own[h][t][:], ALU.subtract
                 )
 
-        def hinge(i, t0=0, t1=PACK):
-            j0, n = PIECES[i]
-            nc.scalar.activation(y[i][:, t0:t1, :], d[i][:, t0:t1, :], ACT.Relu, bias=1.0)
-            nc.sync.dma_start(out_rows[:, t0:t1, j0 : j0 + n], y[i][:, t0:t1, :])
+        def hinge(h, t0, t1):
+            nc.scalar.activation(y[h][:, t0:t1, :], d[h][:, t0:t1, :], ACT.Relu, bias=1.0)
+            nc.sync.dma_start(out_rows[:, t0:t1, h * HALF : (h + 1) * HALF], y[h][:, t0:t1, :])
 
-        def weave(i, on_vector):
-            dst = yb[i][:].rearrange("p (a i) t -> p a t i", i=4)
-            src = d[i][:].rearrange("p t (a i) -> p a t i", i=4)
+        def weave(j0, n, on_vector):
+            yb = sb.tile([P, n, PACK], BF16, name=f"yb{j0}", align_bytes=64)
+            dst = yb[:].rearrange("p (a i) t -> p a t i", i=4)
+            src = d[j0 // HALF][:, :, j0 % HALF : j0 % HALF + n].rearrange("p t (a i) -> p a t i", i=4)
             if on_vector:
                 nc.vector.tensor_scalar(dst, src, 1.0, 0.0, ALU.add, ALU.max)
             else:
                 nc.scalar.activation(dst, src, ACT.Relu, bias=1.0)
+            return yb
 
-        def pack(i):
-            j0, n = PIECES[i]
-            nc.vector.quantize_mx(yw[i][:].bitcast(FP8X4), ys[:, j0 : j0 + n], yb[i][:].rearrange("p n t -> p (n t)"))
-            nc.sync.dma_start(out_words[:, j0 : j0 + n], yw[i][:])
+        def pack(j0, n, yb):
+            yw = sb.tile([P, n], I32, name=f"yw{j0}", tag="own1_3" if j0 == 0 else f"yw{j0}", align_bytes=64)
+            nc.vector.quantize_mx(yw[:].bitcast(FP8X4), ys[:, j0 : j0 + n], yb[:].rearrange("p n t -> p (n t)"))
+            nc.sync.dma_start(out_words[:, j0 : j0 + n], yw[:])
 
         fetch(0)
         hinge(0, 0, 2)
         hinge(0, 2, 4)
-        weave(0, False)
+        yb0 = weave(0, HALF, False)
         fetch(1)
-        hinge(1)
-        fetch(2)
-        hinge(2)
-        weave(1, True)
-        pack(0)
-        weave(2, True)
-        pack(1)
-        pack(2)
+        hinge(1, 0, 2)
+        yb2 = weave(HALF + CH, CH, False)
+        hinge(1, 2, 4)
+        pack(0, HALF, yb0)
+        yb1 = weave(HALF, CH, True)
+        pack(HALF, CH, yb1)
+        pack(HALF + CH, CH, yb2)
         for q in range(4):
             eng = nc.scalar if q % 2 else nc.sync
             eng.dma_start(out_2[0, 4 * q : 4 * q + 4, :].bitcast(I32), ys[32 * q : 32 * q + 4, :].bitcast(I32))

@@ -38,7 +38,7 @@ def tile_picked_candhinge_none_po_kernel(
         xw = sb.tile([P, T], I32, name="xw", align_bytes=64)
         xs = sb.tile([P, T], U8, name="xs", align_bytes=64)
         ww_raw = sb.tile([P, H], I32, name="ww_raw", align_bytes=64)
-        ws_raw = sb.tile([P, H], U8, name="ws_raw", tag="late", align_bytes=64)
+        ws_raw = sb.tile([P, H], U8, name="ws_raw", align_bytes=64)
         gs_sb = sb.tile([P, 1, PACK], F32, name="gs_sb")
 
         nc.vector.memset(xs[:].bitcast(I32), 0)
@@ -57,12 +57,12 @@ def tile_picked_candhinge_none_po_kernel(
         nc.sync.dma_start(gs_sb[:, 0, :], gs.rearrange("(p t) o -> p (t o)", t=PACK))
 
         def deal_words(dst, src):
-            nc.vector.tensor_copy(
+            nc.gpsimd.tensor_copy(
                 dst.rearrange("p (t a i) -> p a t i", t=PACK, i=4), src.rearrange("p (a i t) -> p a t i", t=PACK, i=4)
             )
 
-        def deal_bytes(dst, src):
-            nc.vector.tensor_copy(
+        def deal_bytes(eng, dst, src):
+            eng.tensor_copy(
                 dst.rearrange("p (t a i) -> p a t i", t=PACK, i=16), src.rearrange("p (a i t) -> p a t i", t=PACK, i=16)
             )
 
@@ -75,11 +75,11 @@ def tile_picked_candhinge_none_po_kernel(
 
         nc.vector.tensor_copy(cs_raw[:], xs[:].indirect(cand_sb[:]))
         nc.vector.tensor_copy(qs[:], xs[:].indirect(offs_sb[:]))
-        deal_bytes(cs[:], cs_raw[:])
+        deal_bytes(nc.vector, cs[:], cs_raw[:])
         nc.vector.tensor_copy(qw[:], xw[:].bitcast(U32).indirect(offs_sb[:]))
         deal_words(ww[:], ww_raw[:])
-        deal_bytes(ws[:], ws_raw[:])
-        cw = sb.tile([P, V], U32, name="cw", tag="late", align_bytes=64)
+        deal_bytes(nc.gpsimd, ws[:], ws_raw[:])
+        cw = sb.tile([P, V], U32, name="cw", align_bytes=64)
         nc.vector.tensor_copy(cw[:].rearrange("p (t m) -> p m t", t=PACK), xw[:].bitcast(U32).indirect(cand_sb[:]))
 
         hb = [psum.tile([P, PACK, CH], F32, name=f"hb{c}", tag=f"hb{c}") for c in range(NCH)]
@@ -144,43 +144,52 @@ def tile_picked_candhinge_none_po_kernel(
         d = [sb.tile([P, PACK, HALF], F32, name=f"d{h}", align_bytes=64) for h in range(2)]
         y = [sb.tile([P, PACK, HALF], F32, name=f"y{h}", align_bytes=64) for h in range(2)]
 
-        def fetch(h):
-            for t in range(PACK):
-                nc.vector.tensor_tensor(
-                    d[h][:, t, :], win[t][:].indirect(neg_sb[:, h * HALF // 16 : (h + 1) * HALF // 16]), own[h][t][:], ALU.subtract
-                )
+        def fetch(t, j0, n):
+            h, c0 = divmod(j0, HALF)
+            nc.vector.tensor_tensor(
+                d[h][:, t, c0 : c0 + n], win[t][:].indirect(neg_sb[:, j0 // 16 : (j0 + n) // 16]), own[h][t][:, c0 : c0 + n], ALU.subtract
+            )
 
         def hinge(h, t0, t1):
             nc.scalar.activation(y[h][:, t0:t1, :], d[h][:, t0:t1, :], ACT.Relu, bias=1.0)
             nc.sync.dma_start(out_rows[:, t0:t1, h * HALF : (h + 1) * HALF], y[h][:, t0:t1, :])
 
-        def weave(j0, n, on_vector):
-            yb = sb.tile([P, n, PACK], BF16, name=f"yb{j0}", align_bytes=64)
-            dst = yb[:].rearrange("p (a i) t -> p a t i", i=4)
+        yb = {j0: sb.tile([P, n, PACK], BF16, name=f"yb{j0}", align_bytes=64) for j0, n in ((0, HALF), (HALF, CH), (HALF + CH, CH))}
+
+        def weave(base, j0, n, on_vector):
+            dst = yb[base][:, j0 - base : j0 - base + n, :].rearrange("p (a i) t -> p a t i", i=4)
             src = d[j0 // HALF][:, :, j0 % HALF : j0 % HALF + n].rearrange("p t (a i) -> p a t i", i=4)
             if on_vector:
                 nc.vector.tensor_scalar(dst, src, 1.0, 0.0, ALU.add, ALU.max)
             else:
                 nc.scalar.activation(dst, src, ACT.Relu, bias=1.0)
-            return yb
 
-        def pack(j0, n, yb):
-            yw = sb.tile([P, n], I32, name=f"yw{j0}", tag="own1_3" if j0 == 0 else f"yw{j0}", align_bytes=64)
-            nc.vector.quantize_mx(yw[:].bitcast(FP8X4), ys[:, j0 : j0 + n], yb[:].rearrange("p n t -> p (n t)"))
-            nc.sync.dma_start(out_words[:, j0 : j0 + n], yw[:])
+        def pack(yw, j0, n):
+            nc.vector.quantize_mx(
+                yw[:, j0 % HALF : j0 % HALF + n].bitcast(FP8X4), ys[:, j0 : j0 + n], yb[j0][:].rearrange("p n t -> p (n t)")
+            )
 
-        fetch(0)
+        for t in range(PACK):
+            fetch(t, 0, HALF)
         hinge(0, 0, 2)
         hinge(0, 2, 4)
-        yb0 = weave(0, HALF, False)
-        fetch(1)
+        weave(0, 0, HALF, False)
+        for t in range(PACK - 1):
+            fetch(t, HALF, HALF)
+        fetch(PACK - 1, HALF, CH)
+        fetch(PACK - 1, HALF + CH, CH)
         hinge(1, 0, 2)
-        yb2 = weave(HALF + CH, CH, False)
-        hinge(1, 2, 4)
-        pack(0, HALF, yb0)
-        yb1 = weave(HALF, CH, True)
-        pack(HALF, CH, yb1)
-        pack(HALF + CH, CH, yb2)
+        hinge(1, 2, 3)
+        weave(HALF, HALF, CH, False)
+        hinge(1, 3, 4)
+        yw0 = sb.tile([P, HALF], I32, name="yw0", tag="own1_3", align_bytes=64)
+        pack(yw0, 0, HALF)
+        nc.sync.dma_start(out_words[:, 0:HALF], yw0[:])
+        weave(HALF + CH, HALF + CH, CH, True)
+        yw1 = sb.tile([P, HALF], I32, name="yw1", align_bytes=64)
+        pack(yw1, HALF, CH)
+        pack(yw1, HALF + CH, CH)
+        nc.sync.dma_start(out_words[:, HALF:S], yw1[:])
         for q in range(4):
             eng = nc.scalar if q % 2 else nc.sync
             eng.dma_start(out_2[0, 4 * q : 4 * q + 4, :].bitcast(I32), ys[32 * q : 32 * q + 4, :].bitcast(I32))

from contextlib import ExitStack

import concourse.mybir as mybir

K, T, S, V, H = 512, 2048, 512, 512, 512
FLOPS = 2 * K * H * S + 2 * H * V * S

F32 = mybir.dt.float32
BF16 = mybir.dt.bfloat16
I32 = mybir.dt.int32
U32 = mybir.dt.uint32
U16 = mybir.dt.uint16
U8 = mybir.dt.uint8
FP8X4 = mybir.dt.float8_e4m3fn_x4
ALU = mybir.AluOpType
ACT = mybir.ActivationFunctionType

P = 128
PACK = 4
CH = 128
NCH = S // CH
HALF = S // 2


def tile_picked_candhinge_none_po_kernel(
    tc, x_words, x_scales, w1_words, w1_scales, gs, offs, cand, neg, out_0, out_1, out_2
):
    nc = tc.nc
    with ExitStack() as ctx:
        lists = ctx.enter_context(tc.tile_pool(name="lists", bufs=1))
        sb = ctx.enter_context(tc.tile_pool(name="sb", bufs=1))
        psum = ctx.enter_context(tc.psum_pool(name="psum", bufs=1))

        offs_sb = lists.tile([P, S // 16], U16, name="offs_sb")
        cand_sb = lists.tile([P, V // 16], U16, name="cand_sb")
        neg_sb = lists.tile([P, S // 16], U16, name="neg_sb")

        xw = sb.tile([P, T], I32, name="xw", align_bytes=64)
        xs = sb.tile([P, T], U8, name="xs", align_bytes=64)
        ww_raw = sb.tile([P, H], I32, name="ww_raw", align_bytes=64)
        ws_raw = sb.tile([P, H], U8, name="ws_raw", align_bytes=64)
        gs_sb = sb.tile([P, 1, PACK], F32, name="gs_sb")

        nc.vector.memset(xs[:].bitcast(I32), 0)
        nc.vector.memset(ws_raw[:].bitcast(I32), 0)

        nc.sync.dma_start(cand_sb[:], cand)
        nc.sync.dma_start(offs_sb[:], offs)
        nc.sync.dma_start(neg_sb[:], neg)
        for q in range(4):
            eng = nc.sync if q < 2 else nc.scalar
            eng.dma_start(xs[32 * q : 32 * q + 4, :].bitcast(I32), x_scales[0, 4 * q : 4 * q + 4, :].bitcast(I32))
        nc.sync.dma_start(xw[:], x_words[0].rearrange("p n t -> p (n t)").bitcast(I32))
        nc.sync.dma_start(ww_raw[:], w1_words[0].rearrange("p n t -> p (n t)").bitcast(I32))
        for q in range(4):
            nc.sync.dma_start(ws_raw[32 * q : 32 * q + 4, :].bitcast(I32), w1_scales[0, 4 * q : 4 * q + 4, :].bitcast(I32))
        nc.sync.dma_start(gs_sb[:, 0, :], gs.rearrange("(p t) o -> p (t o)", t=PACK))

        def deal_words(dst, src):
            nc.gpsimd.tensor_copy(
                dst.rearrange("p (t a i) -> p a t i", t=PACK, i=4), src.rearrange("p (a i t) -> p a t i", t=PACK, i=4)
            )

        def deal_bytes(eng, dst, src):
            eng.tensor_copy(
                dst.rearrange("p (t a i) -> p a t i", t=PACK, i=16), src.rearrange("p (a i t) -> p a t i", t=PACK, i=16)
            )

        qs = sb.tile([P, S], U8, name="qs", align_bytes=64)
        cs_raw = sb.tile([P, V], U8, name="cs_raw", align_bytes=64)
        cs = sb.tile([P, V], U8, name="cs", align_bytes=64)
        ww = sb.tile([P, H], I32, name="ww", align_bytes=64)
        ws = sb.tile([P, H], U8, name="ws", align_bytes=64)
        qw = sb.tile([P, S], U32, name="qw", align_bytes=64)

        nc.vector.tensor_copy(cs_raw[:], xs[:].indirect(cand_sb[:]))
        nc.vector.tensor_copy(qs[:], xs[:].indirect(offs_sb[:]))
        deal_bytes(nc.vector, cs[:], cs_raw[:])
        nc.vector.tensor_copy(qw[:], xw[:].bitcast(U32).indirect(offs_sb[:]))
        deal_words(ww[:], ww_raw[:])
        deal_bytes(nc.gpsimd, ws[:], ws_raw[:])
        cw = sb.tile([P, V], U32, name="cw", align_bytes=64)
        nc.vector.tensor_copy(cw[:].rearrange("p (t m) -> p m t", t=PACK), xw[:].bitcast(U32).indirect(cand_sb[:]))

        hb = [psum.tile([P, PACK, CH], F32, name=f"hb{c}", tag=f"hb{c}") for c in range(NCH)]
        for c in range(NCH):
            cols = slice(c * CH, (c + 1) * CH)
            for t in range(PACK):
                m = slice(t * P, (t + 1) * P)
                nc.tensor.matmul_mx(
                    out=hb[c][:, t, :], lhsT=ww[:, m].bitcast(FP8X4), lhsT_scale=ws[:, m],
                    rhs=qw[:, cols].bitcast(FP8X4), rhs_scale=qs[:, cols], start=True, stop=True,
                )

        zb = [sb.tile([P, CH, PACK], BF16, name=f"zb{c}", align_bytes=64) for c in range(NCH)]
        zw = [sb.tile([P, CH], U32, name=f"zw{c}", align_bytes=64) for c in range(NCH)]
        zs = [sb.tile([P, CH], U8, name=f"zs{c}", align_bytes=64) for c in range(NCH)]
        win = [sb.tile([P, S], F32, name=f"win{t}", align_bytes=64) for t in range(PACK)]
        own = [[sb.tile([P, HALF], F32, name=f"own{h}_{t}", tag=f"own{h}_{t}", align_bytes=64) for t in range(PACK)] for h in range(2)]
        acc = {}

        def make_z(c):
            nc.vector.scalar_tensor_tensor(
                zb[c][:], hb[c][:].rearrange("p t n -> p n t"), 0.0, gs_sb[:].to_broadcast([P, CH, PACK]), ALU.max, ALU.mult
            )

        def score(c):
            nc.vector.quantize_mx(zw[c][:].bitcast(FP8X4), zs[c][:], zb[c][:].rearrange("p n t -> p (n t)"))
            if c + 1 < NCH:
                bank = psum.tile([P, PACK, CH], F32, name=f"sbk{c}")
            for t in range(PACK):
                if c + 1 < NCH:
                    acc[c, t] = bank[:, t, :]
                else:
                    last = psum.tile([P, CH], F32, name=f"last{t}", tag=f"hb{t}")
                    acc[c, t] = last[:]
                m = slice(t * P, (t + 1) * P)
                nc.tensor.matmul_mx(
                    out=acc[c, t], lhsT=cw[:, m].bitcast(FP8X4), lhsT_scale=cs[:, m],
                    rhs=zw[c][:].bitcast(FP8X4), rhs_scale=zs[c][:], start=True, stop=True,
                )

        def drain(c, t):
            nc.scalar.activation(win[t][:, c * CH : (c + 1) * CH], acc[c, t], ACT.Copy, scale=0.0625)

        make_z(0)
        for c in range(NCH):
            if c + 1 < NCH:
                make_z(c + 1)
            score(c)
        for c in range(2):
            for t in range(PACK):
                drain(c, t)
        for t in range(PACK):
            nc.vector.tensor_copy(own[0][t][:], win[t][:, 0:HALF])
        for t in range(PACK):
            drain(2, t)
            drain(3, t)
            nc.sync.dma_start(own[1][t][:], win[t][:, HALF:S])

        ys = sb.tile([P, S], U8, name="ys", align_bytes=64)
        out_rows = out_0.rearrange("(p t) j -> p t j", t=PACK)
        out_words = out_1[0].rearrange("p n t -> p (n t)").bitcast(I32)
        d = [sb.tile([P, PACK, HALF], F32, name=f"d{h}", align_bytes=64) for h in range(2)]
        y = [sb.tile([P, PACK, HALF], F32, name=f"y{h}", align_bytes=64) for h in range(2)]

        def fetch(t, j0, n):
            h, c0 = divmod(j0, HALF)
            nc.vector.tensor_tensor(
                d[h][:, t, c0 : c0 + n], win[t][:].indirect(neg_sb[:, j0 // 16 : (j0 + n) // 16]), own[h][t][:, c0 : c0 + n], ALU.subtract
            )

        def hinge(h, t0, t1):
            nc.scalar.activation(y[h][:, t0:t1, :], d[h][:, t0:t1, :], ACT.Relu, bias=1.0)
            nc.sync.dma_start(out_rows[:, t0:t1, h * HALF : (h + 1) * HALF], y[h][:, t0:t1, :])

        yb = {j0: sb.tile([P, n, PACK], BF16, name=f"yb{j0}", align_bytes=64) for j0, n in ((0, HALF), (HALF, CH), (HALF + CH, CH))}

        def weave(base, j0, n, on_vector):
            dst = yb[base][:, j0 - base : j0 - base + n, :].rearrange("p (a i) t -> p a t i", i=4)
            src = d[j0 // HALF][:, :, j0 % HALF : j0 % HALF + n].rearrange("p t (a i) -> p a t i", i=4)
            if on_vector:
                nc.vector.tensor_scalar(dst, src, 1.0, 0.0, ALU.add, ALU.max)
            else:
                nc.scalar.activation(dst, src, ACT.Relu, bias=1.0)

        def pack(yw, j0, n):
            nc.vector.quantize_mx(
                yw[:, j0 % HALF : j0 % HALF + n].bitcast(FP8X4), ys[:, j0 : j0 + n], yb[j0][:].rearrange("p n t -> p (n t)")
            )

        for t in range(PACK):
            fetch(t, 0, HALF)
        hinge(0, 0, 2)
        hinge(0, 2, 4)
        weave(0, 0, HALF, False)
        for t in range(PACK - 1):
            fetch(t, HALF, HALF)
        fetch(PACK - 1, HALF, CH)
        fetch(PACK - 1, HALF + CH, CH)
        hinge(1, 0, 2)
        hinge(1, 2, 3)
        weave(HALF, HALF, CH, False)
        hinge(1, 3, 4)
        yw0 = sb.tile([P, HALF], I32, name="yw0", tag="own1_3", align_bytes=64)
        pack(yw0, 0, HALF)
        nc.sync.dma_start(out_words[:, 0:HALF], yw0[:])
        weave(HALF + CH, HALF + CH, CH, True)
        yw1 = sb.tile([P, HALF], I32, name="yw1", align_bytes=64)
        pack(yw1, HALF, CH)
        pack(yw1, HALF + CH, CH)
        nc.sync.dma_start(out_words[:, HALF:S], yw1[:])
        for q in range(4):
            eng = nc.scalar if q % 2 else nc.sync
            eng.dma_start(out_2[0, 4 * q : 4 * q + 4, :].bitcast(I32), ys[32 * q : 32 * q + 4, :].bitcast(I32))
